import numpy as np
import ml_dtypes


def mxq(x, axis, fmt="e4m3"):
    dtype, down = {"e4m3": (ml_dtypes.float8_e4m3fn, 7), "e5m2": (ml_dtypes.float8_e5m2, 14)}[fmt]
    v = np.moveaxis(np.asarray(x, np.float32).astype(ml_dtypes.bfloat16).astype(np.float64), axis, -1)
    blocks = v.reshape(v.shape[:-1] + (-1, 32))
    amax = np.abs(blocks).max(-1, keepdims=True)
    byte = np.maximum(np.where(amax > 0, np.frexp(amax)[1] - 1 + 127, 0) - down, 1)
    scale = np.exp2(byte - 127.0)
    codes = (blocks / scale).astype(np.float32).astype(dtype).astype(np.float64)
    return np.moveaxis((codes * scale).reshape(v.shape), -1, axis)


WIDE = False


def mx_kscale(k):
    if not WIDE:
        return np.ones(k)
    levels = np.array([10, -10, 5, -5, 0])
    if k % 512:
        return np.exp2(np.random.permutation(np.resize(levels, k // 32))).repeat(32)
    a = np.empty((k // 512, 16))
    for p in range(k // 512):
        a[p, :8] = np.random.permutation(np.resize(levels, 8))
        for g in range(8):
            far = levels[np.abs(levels - a[p, g]) >= 10]
            a[p, g + 8] = far[np.random.randint(len(far))]
    return np.exp2(a.ravel()).repeat(32)


def f64(x):
    return np.asarray(x).astype(np.float64)


def striped(idx):
    return np.tile(idx.reshape(-1, 16).T, (8, 1)).astype(np.uint16)


def unstriped(offs):
    return offs[:16].T.reshape(-1).astype(np.int64)


def pack_weight(w):
    k, n = w.shape
    w = f64(np.asarray(w, np.float32).astype(ml_dtypes.bfloat16)).reshape(k // 32, 32, n)
    amax = np.abs(w).max(1)
    byte = np.clip(np.where(amax > 0, np.frexp(amax)[1] - 1 + 127 - 7, 1), 1, 254)
    scaled = (w * np.exp2(127.0 - byte)[:, None, :]).reshape(k, n).astype(np.float32)
    words = np.ascontiguousarray(scaled.reshape(k // 512, 128, 4, n).transpose(0, 1, 3, 2)).astype(ml_dtypes.float8_e4m3fn).view(np.uint8)
    return words, np.ascontiguousarray(byte.astype(np.uint8).reshape(k // 512, 16, n))


def unpack_weight(words, scales):
    g, p, n, _ = words.shape
    vals = np.ascontiguousarray(words).view(ml_dtypes.float8_e4m3fn).astype(np.float64) * np.repeat(np.exp2(scales.astype(np.float64) - 127.0), 8, axis=1)[..., None]
    return vals.transpose(0, 1, 3, 2).reshape(g * 512, n)


def relu(v):
    return np.maximum(v, 0.0)


K, T, D, S, V, H, N = 1024, 2048, 2, 1024, 512, 512, 128


def setup_inputs():
    n = np.random.standard_normal
    s = mx_kscale(K)[:, None]
    u = mx_kscale(H)
    packed = pack_weight(n((K, T)) * s)
    return {
        "x_words": packed[0],
        "x_scales": packed[1],
        "w1": (n((K, H)) / np.sqrt(K) / s * u).astype(np.float32),
        "w2": (n((H, N)) / np.sqrt(H) / u[:, None]).astype(np.float32),
        "gate": np.tile(np.random.uniform(0.5, 1.5, V), (N, 1)).astype(np.float32),
        "offs": striped(np.random.permutation(T)[:S]),
        "pos1": striped(np.random.permutation(2 * V)[:V]),
    }


def reference(x_words, x_scales, w1, w2, gate, offs, pos1):
    h = relu(mxq(f64(w1), 0, "e4m3").T @ unpack_weight(x_words, x_scales)[:, unstriped(offs)])
    z = h.reshape(H, V, D).max(axis=2)
    out = np.zeros((N, 2 * V))
    out[:, unstriped(pos1)] = f64(gate) * (mxq(f64(w2), 0, "e4m3").T @ mxq(z, 0, "e4m3"))
    return out

@@ -1,0 +1,220 @@
+from contextlib import ExitStack
+
+import concourse.mybir as mybir
+
+K, T, D, S, V, H, N = 1024, 2048, 2, 1024, 512, 512, 128
+FLOPS = 2 * K * H * S + 2 * H * N * V
+
+F32 = mybir.dt.float32
+BF16 = mybir.dt.bfloat16
+I32 = mybir.dt.int32
+U32 = mybir.dt.uint32
+U16 = mybir.dt.uint16
+U8 = mybir.dt.uint8
+FP8X4 = mybir.dt.float8_e4m3fn_x4
+ACT = mybir.ActivationFunctionType
+ALU = mybir.AluOpType
+
+P = 128
+PACK = 4
+K_PASS = P * PACK
+BANK_TOKENS = 128
+BANKS = S // BANK_TOKENS
+H_BANKS = 6
+CHUNK_TOKENS = 256
+CHUNKS = S // CHUNK_TOKENS
+CHUNK_V = CHUNK_TOKENS // D
+BANK_V = BANK_TOKENS // D
+M_SPLIT = 64
+
+
+def tile_picked_vpool_relu_p_kernel(
+    tc, x_words, x_scales, w1, w2, gate, offs, pos1, out
+):
+    nc = tc.nc
+    with ExitStack() as ctx:
+        keep = ctx.enter_context(tc.tile_pool(name="keep", bufs=1))
+        reuse = ctx.enter_context(tc.tile_pool(name="reuse", bufs=1))
+        hpsum = ctx.enter_context(tc.psum_pool(name="hpsum", bufs=H_BANKS))
+        ypsum = ctx.enter_context(tc.psum_pool(name="ypsum", bufs=2))
+
+        offs_sb = keep.tile([P, S // 16], U16, name="offs_sb")
+        pos_sb = keep.tile([P, V // 16], U16, name="pos_sb")
+        nc.sync.dma_start(offs_sb[:], offs)
+
+        scale_table = keep.tile([P, T], U8, name="scale_table", align_bytes=64)
+        nc.vector.memset(scale_table[:].bitcast(I32), 0)
+
+        word_table = [keep.tile([P, T], U32, name="word_table%d" % o, tag="word_table%d" % o, align_bytes=64) for o in range(2)]
+        w1_raw = [keep.tile([P, PACK, H], F32, name="w1_raw%d" % o, align_bytes=64) for o in range(2)]
+
+        def load_words(o):
+            nc.sync.dma_start(
+                out=word_table[o][:].bitcast(I32),
+                in_=x_words[o].rearrange("p c r -> p (c r)").bitcast(I32),
+            )
+
+        def load_w1(o):
+            nc.sync.dma_start(
+                out=w1_raw[o][:],
+                in_=w1[o * K_PASS : (o + 1) * K_PASS, :].rearrange("(p j) c -> p j c", j=PACK),
+            )
+
+        load_words(0)
+        for q in range(4):
+            nc.sync.dma_start(
+                out=scale_table[32 * q : 32 * q + 8, :].bitcast(I32),
+                in_=x_scales[:, 4 * q : 4 * q + 4, :].bitcast(I32),
+            )
+        load_w1(1)
+        load_w1(0)
+        load_words(1)
+        w2_raw = keep.tile([P, PACK, N], F32, name="w2_raw", align_bytes=64)
+        nc.sync.dma_start(out=w2_raw[:], in_=w2.rearrange("(p j) n -> p j n", j=PACK))
+        nc.sync.dma_start(pos_sb[:], pos1)
+        gate_sb = keep.tile([P, V], F32, name="gate_sb", align_bytes=64)
+        nc.sync.dma_start(out=gate_sb[:], in_=gate)
+
+        frame = keep.tile([P, 2 * V], F32, name="frame", align_bytes=64)
+        nc.vector.memset(frame[:], 0.0)
+
+        words0 = keep.tile([P, S], U32, name="words0", align_bytes=64)
+        nc.vector.tensor_copy(words0[:], word_table[0][:].indirect(offs_sb[:]))
+        x_scale = keep.tile([P, S], U8, name="x_scale", align_bytes=64)
+        nc.vector.tensor_copy(x_scale[:], scale_table[:].indirect(offs_sb[:]))
+
+        w1_bf = [
+            reuse.tile([P, PACK, P, PACK], BF16, name="w1_bf0", offset=0, align_bytes=64),
+            keep.tile([P, PACK, P, PACK], BF16, name="w1_bf1", align_bytes=64),
+        ]
+        w1_codes = [keep.tile([P, H], U32, name="w1_codes%d" % o, align_bytes=64) for o in range(2)]
+        w1_scale = [keep.tile([P, H], U8, name="w1_scale%d" % o, align_bytes=64) for o in range(2)]
+
+        def deal_views(o, m0, m1):
+            dst = w1_bf[o][:, :, m0:m1, :].rearrange("p t m j -> p m j t")
+            src = w1_raw[o][:, :, PACK * m0 : PACK * m1].rearrange("p j (m t) -> p m j t", t=PACK)
+            return dst, src
+
+        def quantize_w1(o):
+            nc.vector.quantize_mx(
+                out=w1_codes[o][:].bitcast(FP8X4),
+                scales=w1_scale[o][:],
+                in_=w1_bf[o][:].rearrange("p t m j -> p (t m j)"),
+            )
+
+        dst, src = deal_views(1, 0, P)
+        nc.scalar.activation(dst, src, ACT.Copy)
+        quantize_w1(1)
+        dst, src = deal_views(0, 0, M_SPLIT)
+        nc.scalar.activation(dst, src, ACT.Copy)
+        dst, src = deal_views(0, M_SPLIT, P)
+        nc.vector.tensor_copy(dst, src)
+        quantize_w1(0)
+
+        words1 = [
+            reuse.tile([P, CHUNK_TOKENS], U32, name="words1_%d" % c, offset=4 * CHUNK_TOKENS * c, align_bytes=64)
+            for c in range(CHUNKS)
+        ]
+        for c in range(CHUNKS):
+            cols = CHUNK_TOKENS // 16
+            nc.vector.tensor_copy(words1[c][:], word_table[1][:].indirect(offs_sb[:, c * cols : (c + 1) * cols]))
+
+        w2_bf = keep.tile([P, N, PACK], BF16, name="w2_bf", align_bytes=64)
+        nc.scalar.activation(
+            w2_bf[:].rearrange("p (c i) j -> p c j i", i=4),
+            w2_raw[:].rearrange("p j (c i) -> p c j i", i=4),
+            ACT.Copy,
+        )
+        w2_codes = keep.tile([P, N], U32, name="w2_codes", tag="word_table1", align_bytes=64)
+        w2_scale = keep.tile([P, N], U8, name="w2_scale", align_bytes=64)
+        nc.vector.quantize_mx(
+            out=w2_codes[:].bitcast(FP8X4), scales=w2_scale[:], in_=w2_bf[:].rearrange("p n j -> p (n j)")
+        )
+
+        def first_pass(bank, b, t, o):
+            tok = slice(b * BANK_TOKENS, (b + 1) * BANK_TOKENS)
+            if o == 0:
+                rhs = words0[:, tok]
+            else:
+                c, half = divmod(b, CHUNK_TOKENS // BANK_TOKENS)
+                rhs = words1[c][:, half * BANK_TOKENS : (half + 1) * BANK_TOKENS]
+            nc.tensor.matmul_mx(
+                out=bank[:, t, :],
+                lhsT=w1_codes[o][:, t * P : (t + 1) * P].bitcast(FP8X4),
+                lhsT_scale=w1_scale[o][:, t * P : (t + 1) * P],
+                rhs=rhs.bitcast(FP8X4),
+                rhs_scale=x_scale[4 * o : P, tok],
+                start=(o == 0),
+                stop=(o == 1),
+            )
+
+        banks = []
+        for b in range(H_BANKS):
+            bank = hpsum.tile([P, PACK, BANK_TOKENS], F32, name="h_bank")
+            banks.append(bank)
+            first_pass(bank, b, 0, 0)
+
+        y_bank = {}
+        h_bf = [keep.tile([P, D, CHUNK_V, PACK], BF16, name="h_bf%d" % c, tag="h_bf%d" % c, align_bytes=64) for c in range(CHUNKS)]
+        z_bf = [keep.tile([P, CHUNK_V * PACK], BF16, name="z_bf%d" % c, align_bytes=64) for c in range(CHUNKS)]
+        z_codes = [keep.tile([P, CHUNK_V], U32, name="z_codes%d" % c, align_bytes=64) for c in range(CHUNKS)]
+        z_scale = [keep.tile([P, CHUNK_V], U8, name="z_scale%d" % c, align_bytes=64) for c in range(CHUNKS)]
+        y_sb = {}
+
+        def first_layer(b):
+            if b < H_BANKS:
+                bank = banks[b]
+            else:
+                bank = hpsum.tile([P, PACK, BANK_TOKENS], F32, name="h_bank")
+                first_pass(bank, b, 0, 0)
+            first_pass(bank, b, 0, 1)
+            for t in range(1, PACK):
+                first_pass(bank, b, t, 0)
+                first_pass(bank, b, t, 1)
+            c, half = divmod(b, CHUNK_TOKENS // BANK_TOKENS)
+            nc.scalar.activation(
+                h_bf[c][:, :, half * BANK_V : (half + 1) * BANK_V, :],
+                bank[:].rearrange("p t (v d) -> p d v t", d=D),
+                ACT.Relu,
+            )
+
+        def pool_and_multiply(c):
+            nc.vector.tensor_tensor(
+                z_bf[c][:],
+                h_bf[c][:, 0].rearrange("p v t -> p (v t)"),
+                h_bf[c][:, 1].rearrange("p v t -> p (v t)"),
+                ALU.max,
+            )
+            nc.vector.quantize_mx(out=z_codes[c][:].bitcast(FP8X4), scales=z_scale[c][:], in_=z_bf[c][:])
+            y_bank[c] = ypsum.tile([P, CHUNK_V], F32, name="y_bank")
+            nc.tensor.matmul_mx(
+                out=y_bank[c][:],
+                lhsT=w2_codes[:].bitcast(FP8X4),
+                lhsT_scale=w2_scale[:],
+                rhs=z_codes[c][:].bitcast(FP8X4),
+                rhs_scale=z_scale[c][:],
+                start=True,
+                stop=True,
+            )
+
+        def place(c):
+            y_sb[c] = keep.tile([P, CHUNK_V], F32, name="y_sb%d" % c, tag="h_bf%d" % ((c + 1) % CHUNKS), align_bytes=64)
+            nc.scalar.copy(y_sb[c][:], y_bank[c][:])
+            cols = CHUNK_V // 16
+            nc.vector.tensor_tensor(
+                frame[:].indirect(pos_sb[:, c * cols : (c + 1) * cols]),
+                y_sb[c][:],
+                gate_sb[:, c * CHUNK_V : (c + 1) * CHUNK_V],
+                ALU.mult,
+            )
+
+        for c in range(CHUNKS + 2):
+            if c < CHUNKS:
+                first_layer(2 * c)
+                first_layer(2 * c + 1)
+            if 1 <= c <= CHUNKS:
+                pool_and_multiply(c - 1)
+            if c >= 2:
+                place(c - 2)
+
+        nc.sync.dma_start(out=out, in_=frame[:])

@@ -20,12 +20,13 @@ PACK = 4
 K_PASS = P * PACK
 BANK_TOKENS = 128
 BANKS = S // BANK_TOKENS
-H_BANKS = 6
 CHUNK_TOKENS = 256
 CHUNKS = S // CHUNK_TOKENS
 CHUNK_V = CHUNK_TOKENS // D
 BANK_V = BANK_TOKENS // D
-M_SPLIT = 64
+SCALAR_TILES = 2
+GATHER_PIECES = ((0, 256), (256, 512), (512, 1024))
+GROUPS = ((0, 128, 3, "y_first"), (128, 384, 5, "h_bf3"), (384, 512, 1, "y_last"))
 
 
 def tile_picked_vpool_relu_p_kernel(
@@ -35,18 +36,16 @@ def tile_picked_vpool_relu_p_kernel(
     with ExitStack() as ctx:
         keep = ctx.enter_context(tc.tile_pool(name="keep", bufs=1))
         reuse = ctx.enter_context(tc.tile_pool(name="reuse", bufs=1))
-        hpsum = ctx.enter_context(tc.psum_pool(name="hpsum", bufs=H_BANKS))
-        ypsum = ctx.enter_context(tc.psum_pool(name="ypsum", bufs=2))
+        psum = ctx.enter_context(tc.psum_pool(name="psum", bufs=1))
 
         offs_sb = keep.tile([P, S // 16], U16, name="offs_sb")
         pos_sb = keep.tile([P, V // 16], U16, name="pos_sb")
-        nc.sync.dma_start(offs_sb[:], offs)
 
-        scale_table = keep.tile([P, T], U8, name="scale_table", align_bytes=64)
+        scale_table = keep.tile([P, T], U8, name="scale_table", tag="scale_table", align_bytes=64)
         nc.vector.memset(scale_table[:].bitcast(I32), 0)
 
         word_table = [keep.tile([P, T], U32, name="word_table%d" % o, tag="word_table%d" % o, align_bytes=64) for o in range(2)]
-        w1_raw = [keep.tile([P, PACK, H], F32, name="w1_raw%d" % o, align_bytes=64) for o in range(2)]
+        w1_raw = [keep.tile([P, PACK, H], F32, name="w1_raw%d" % o, tag="w1_raw%d" % o, align_bytes=64) for o in range(2)]
 
         def load_words(o):
             nc.sync.dma_start(
@@ -61,6 +60,8 @@ def tile_picked_vpool_relu_p_kernel(
             )
 
         load_words(0)
+        nc.sync.dma_start(offs_sb[:], offs)
+        nc.sync.dma_start(pos_sb[:], pos1)
         for q in range(4):
             nc.sync.dma_start(
                 out=scale_table[32 * q : 32 * q + 8, :].bitcast(I32),
@@ -70,8 +71,9 @@ def tile_picked_vpool_relu_p_kernel(
         load_w1(0)
         load_words(1)
         w2_raw = keep.tile([P, PACK, N], F32, name="w2_raw", align_bytes=64)
-        nc.sync.dma_start(out=w2_raw[:], in_=w2.rearrange("(p j) n -> p j n", j=PACK))
-        nc.sync.dma_start(pos_sb[:], pos1)
+        w2_rows = w2.rearrange("(b t r) n -> t b r n", t=PACK, r=8)
+        for t in range(PACK):
+            nc.sync.dma_start(out=w2_raw[:, t, :], in_=w2_rows[t])
         gate_sb = keep.tile([P, V], F32, name="gate_sb", align_bytes=64)
         nc.sync.dma_start(out=gate_sb[:], in_=gate)
 
@@ -80,46 +82,48 @@ def tile_picked_vpool_relu_p_kernel(
 
         words0 = keep.tile([P, S], U32, name="words0", align_bytes=64)
         nc.vector.tensor_copy(words0[:], word_table[0][:].indirect(offs_sb[:]))
-        x_scale = keep.tile([P, S], U8, name="x_scale", align_bytes=64)
+        x_scale = keep.tile([P, S], U8, name="x_scale", tag="word_table0", align_bytes=64)
         nc.vector.tensor_copy(x_scale[:], scale_table[:].indirect(offs_sb[:]))
 
         w1_bf = [
             reuse.tile([P, PACK, P, PACK], BF16, name="w1_bf0", offset=0, align_bytes=64),
-            keep.tile([P, PACK, P, PACK], BF16, name="w1_bf1", align_bytes=64),
+            keep.tile([P, PACK, P, PACK], BF16, name="w1_bf1", tag="w1_bf1", align_bytes=64),
         ]
-        w1_codes = [keep.tile([P, H], U32, name="w1_codes%d" % o, align_bytes=64) for o in range(2)]
+        w1_codes = {}
         w1_scale = [keep.tile([P, H], U8, name="w1_scale%d" % o, align_bytes=64) for o in range(2)]
 
-        def deal_views(o, m0, m1):
-            dst = w1_bf[o][:, :, m0:m1, :].rearrange("p t m j -> p m j t")
-            src = w1_raw[o][:, :, PACK * m0 : PACK * m1].rearrange("p j (m t) -> p m j t", t=PACK)
+        def deal_views(o, t):
+            dst = w1_bf[o][:, t].rearrange("p (b h i) j -> p b h j i", h=2, i=4)
+            src = w1_raw[o][:].rearrange("p j (b t h i) -> p t b h j i", t=PACK, h=2, i=4)[:, t]
             return dst, src
 
-        def quantize_w1(o):
+        def quantize_w1(o, tag):
+            w1_codes[o] = keep.tile([P, H], U32, name="w1_codes%d" % o, tag=tag, align_bytes=64)
             nc.vector.quantize_mx(
                 out=w1_codes[o][:].bitcast(FP8X4),
                 scales=w1_scale[o][:],
                 in_=w1_bf[o][:].rearrange("p t m j -> p (t m j)"),
             )
 
-        dst, src = deal_views(1, 0, P)
-        nc.scalar.activation(dst, src, ACT.Copy)
-        quantize_w1(1)
-        dst, src = deal_views(0, 0, M_SPLIT)
-        nc.scalar.activation(dst, src, ACT.Copy)
-        dst, src = deal_views(0, M_SPLIT, P)
-        nc.vector.tensor_copy(dst, src)
-        quantize_w1(0)
+        for t in range(PACK):
+            nc.scalar.copy(*deal_views(1, t))
+        quantize_w1(1, "scale_table")
+        for t in range(PACK):
+            if t < SCALAR_TILES:
+                nc.scalar.copy(*deal_views(0, t))
+            else:
+                nc.vector.tensor_copy(*deal_views(0, t))
+        quantize_w1(0, "w1_bf1")
 
-        words1 = [
-            reuse.tile([P, CHUNK_TOKENS], U32, name="words1_%d" % c, offset=4 * CHUNK_TOKENS * c, align_bytes=64)
-            for c in range(CHUNKS)
-        ]
-        for c in range(CHUNKS):
-            cols = CHUNK_TOKENS // 16
-            nc.vector.tensor_copy(words1[c][:], word_table[1][:].indirect(offs_sb[:, c * cols : (c + 1) * cols]))
+        words1 = []
+        for first, last in GATHER_PIECES:
+            piece = reuse.tile(
+                [P, last - first], U32, name="words1_%d" % first, offset=4 * first, align_bytes=64
+            )
+            nc.vector.tensor_copy(piece[:], word_table[1][:].indirect(offs_sb[:, first // 16 : last // 16]))
+            words1.extend(piece[:, n : n + BANK_TOKENS] for n in range(0, last - first, BANK_TOKENS))
 
-        w2_bf = keep.tile([P, N, PACK], BF16, name="w2_bf", align_bytes=64)
+        w2_bf = keep.tile([P, N, PACK], BF16, name="w2_bf", tag="w1_raw0", align_bytes=64)
         nc.scalar.activation(
             w2_bf[:].rearrange("p (c i) j -> p c j i", i=4),
             w2_raw[:].rearrange("p j (c i) -> p c j i", i=4),
@@ -136,8 +140,7 @@ def tile_picked_vpool_relu_p_kernel(
             if o == 0:
                 rhs = words0[:, tok]
             else:
-                c, half = divmod(b, CHUNK_TOKENS // BANK_TOKENS)
-                rhs = words1[c][:, half * BANK_TOKENS : (half + 1) * BANK_TOKENS]
+                rhs = words1[b]
             nc.tensor.matmul_mx(
                 out=bank[:, t, :],
                 lhsT=w1_codes[o][:, t * P : (t + 1) * P].bitcast(FP8X4),
@@ -148,73 +151,76 @@ def tile_picked_vpool_relu_p_kernel(
                 stop=(o == 1),
             )
 
+        warm_bank = psum.tile([P, 512], F32, name="warm_bank", tag="bank%d" % (BANKS - 1))
+        for i in range(4):
+            nc.tensor.matmul_mx(
+                out=warm_bank[:],
+                lhsT=words0[:, 0:P].bitcast(FP8X4),
+                lhsT_scale=x_scale[:, 0:P],
+                rhs=words0[:, 0:512].bitcast(FP8X4),
+                rhs_scale=x_scale[:, 0:512],
+                start=True,
+                stop=True,
+            )
+
         banks = []
-        for b in range(H_BANKS):
-            bank = hpsum.tile([P, PACK, BANK_TOKENS], F32, name="h_bank")
+        for b in range(BANKS):
+            bank = psum.tile([P, PACK, BANK_TOKENS], F32, name="h_bank%d" % b, tag="bank%d" % b)
             banks.append(bank)
             first_pass(bank, b, 0, 0)
 
-        y_bank = {}
         h_bf = [keep.tile([P, D, CHUNK_V, PACK], BF16, name="h_bf%d" % c, tag="h_bf%d" % c, align_bytes=64) for c in range(CHUNKS)]
-        z_bf = [keep.tile([P, CHUNK_V * PACK], BF16, name="z_bf%d" % c, align_bytes=64) for c in range(CHUNKS)]
-        z_codes = [keep.tile([P, CHUNK_V], U32, name="z_codes%d" % c, align_bytes=64) for c in range(CHUNKS)]
-        z_scale = [keep.tile([P, CHUNK_V], U8, name="z_scale%d" % c, align_bytes=64) for c in range(CHUNKS)]
-        y_sb = {}
+        z_codes = keep.tile([P, V], U32, name="z_codes", align_bytes=64)
+        z_scale = keep.tile([P, V], U8, name="z_scale", align_bytes=64)
 
         def first_layer(b):
-            if b < H_BANKS:
-                bank = banks[b]
-            else:
-                bank = hpsum.tile([P, PACK, BANK_TOKENS], F32, name="h_bank")
-                first_pass(bank, b, 0, 0)
+            bank = banks[b]
             first_pass(bank, b, 0, 1)
             for t in range(1, PACK):
                 first_pass(bank, b, t, 0)
                 first_pass(bank, b, t, 1)
             c, half = divmod(b, CHUNK_TOKENS // BANK_TOKENS)
             nc.scalar.activation(
-                h_bf[c][:, :, half * BANK_V : (half + 1) * BANK_V, :],
-                bank[:].rearrange("p t (v d) -> p d v t", d=D),
+                h_bf[c][:, :, half * BANK_V : (half + 1) * BANK_V, :].rearrange("p d v t -> p v t d"),
+                bank[:].rearrange("p t (v d) -> p v t d", d=D),
                 ACT.Relu,
             )
 
-        def pool_and_multiply(c):
+        def pool(c):
+            z_bf = keep.tile([P, CHUNK_V * PACK], BF16, name="z_bf%d" % c, align_bytes=64)
             nc.vector.tensor_tensor(
-                z_bf[c][:],
+                z_bf[:],
                 h_bf[c][:, 0].rearrange("p v t -> p (v t)"),
                 h_bf[c][:, 1].rearrange("p v t -> p (v t)"),
                 ALU.max,
             )
-            nc.vector.quantize_mx(out=z_codes[c][:].bitcast(FP8X4), scales=z_scale[c][:], in_=z_bf[c][:])
-            y_bank[c] = ypsum.tile([P, CHUNK_V], F32, name="y_bank")
+            cols = slice(c * CHUNK_V, (c + 1) * CHUNK_V)
+            nc.vector.quantize_mx(out=z_codes[:, cols].bitcast(FP8X4), scales=z_scale[:, cols], in_=z_bf[:])
+
+        def place(first, last, b, host):
+            y_bank = psum.tile([P, last - first], F32, name="y_bank%d" % first, tag="bank%d" % b)
             nc.tensor.matmul_mx(
-                out=y_bank[c][:],
+                out=y_bank[:],
                 lhsT=w2_codes[:].bitcast(FP8X4),
                 lhsT_scale=w2_scale[:],
-                rhs=z_codes[c][:].bitcast(FP8X4),
-                rhs_scale=z_scale[c][:],
+                rhs=z_codes[:, first:last].bitcast(FP8X4),
+                rhs_scale=z_scale[:, first:last],
                 start=True,
                 stop=True,
             )
-
-        def place(c):
-            y_sb[c] = keep.tile([P, CHUNK_V], F32, name="y_sb%d" % c, tag="h_bf%d" % ((c + 1) % CHUNKS), align_bytes=64)
-            nc.scalar.copy(y_sb[c][:], y_bank[c][:])
-            cols = CHUNK_V // 16
+            y_sb = keep.tile([P, last - first], F32, name="y_sb%d" % first, tag=host, align_bytes=64)
+            nc.scalar.copy(y_sb[:], y_bank[:])
             nc.vector.tensor_tensor(
-                frame[:].indirect(pos_sb[:, c * cols : (c + 1) * cols]),
-                y_sb[c][:],
-                gate_sb[:, c * CHUNK_V : (c + 1) * CHUNK_V],
-                ALU.mult,
+                frame[:].indirect(pos_sb[:, first // 16 : last // 16]), y_sb[:], gate_sb[:, first:last], ALU.mult
             )
 
-        for c in range(CHUNKS + 2):
-            if c < CHUNKS:
-                first_layer(2 * c)
-                first_layer(2 * c + 1)
-            if 1 <= c <= CHUNKS:
-                pool_and_multiply(c - 1)
-            if c >= 2:
-                place(c - 2)
+        for c in range(CHUNKS):
+            first_layer(2 * c)
+            first_layer(2 * c + 1)
+            pool(c)
+            if c == 1:
+                place(*GROUPS[0])
+        place(*GROUPS[1])
+        place(*GROUPS[2])
 
         nc.sync.dma_start(out=out, in_=frame[:])

@@ -18,15 +18,23 @@ ALU = mybir.AluOpType
 P = 128
 PACK = 4
 K_PASS = P * PACK
+PASSES = K // K_PASS
+QUADRANT = 32
+SCALE_ROWS = 4
+BLOCK_PARTITIONS = 8
+LINE = 4
+LIST_ROWS = 16
+WORD_BYTES = 4
+
 BANK_TOKENS = 128
 BANKS = S // BANK_TOKENS
-CHUNK_TOKENS = 256
-CHUNKS = S // CHUNK_TOKENS
-CHUNK_V = CHUNK_TOKENS // D
 BANK_V = BANK_TOKENS // D
+CHUNK_V = 2 * BANK_V
+CHUNKS = V // CHUNK_V
+WARM_N = 512
+
 SCALAR_TILES = 2
 GATHER_PIECES = ((0, 256), (256, 512), (512, 1024))
-GROUPS = ((0, 128, 3, "y_first"), (128, 384, 5, "h_bf3"), (384, 512, 1, "y_last"))
 
 
 def tile_picked_vpool_relu_p_kernel(
@@ -38,14 +46,17 @@ def tile_picked_vpool_relu_p_kernel(
         reuse = ctx.enter_context(tc.tile_pool(name="reuse", bufs=1))
         psum = ctx.enter_context(tc.psum_pool(name="psum", bufs=1))
 
-        offs_sb = keep.tile([P, S // 16], U16, name="offs_sb")
-        pos_sb = keep.tile([P, V // 16], U16, name="pos_sb")
+        offs_sb = keep.tile([P, S // LIST_ROWS], U16, name="offs_sb")
+        pos_sb = keep.tile([P, V // LIST_ROWS], U16, name="pos_sb")
 
         scale_table = keep.tile([P, T], U8, name="scale_table", tag="scale_table", align_bytes=64)
         nc.vector.memset(scale_table[:].bitcast(I32), 0)
 
-        word_table = [keep.tile([P, T], U32, name="word_table%d" % o, tag="word_table%d" % o, align_bytes=64) for o in range(2)]
-        w1_raw = [keep.tile([P, PACK, H], F32, name="w1_raw%d" % o, tag="w1_raw%d" % o, align_bytes=64) for o in range(2)]
+        word_table = [
+            keep.tile([P, T], U32, name="word_table%d" % o, tag="word_table%d" % o, align_bytes=64)
+            for o in range(PASSES)
+        ]
+        w1_raw = [keep.tile([P, PACK, H], F32, name="w1_raw%d" % o, align_bytes=64) for o in range(PASSES)]
 
         def load_words(o):
             nc.sync.dma_start(
@@ -62,16 +73,16 @@ def tile_picked_vpool_relu_p_kernel(
         load_words(0)
         nc.sync.dma_start(offs_sb[:], offs)
         nc.sync.dma_start(pos_sb[:], pos1)
-        for q in range(4):
+        for q in range(P // QUADRANT):
             nc.sync.dma_start(
-                out=scale_table[32 * q : 32 * q + 8, :].bitcast(I32),
-                in_=x_scales[:, 4 * q : 4 * q + 4, :].bitcast(I32),
+                out=scale_table[QUADRANT * q : QUADRANT * q + PASSES * SCALE_ROWS, :].bitcast(I32),
+                in_=x_scales[:, SCALE_ROWS * q : SCALE_ROWS * (q + 1), :].bitcast(I32),
             )
-        load_w1(1)
         load_w1(0)
+        load_w1(1)
         load_words(1)
         w2_raw = keep.tile([P, PACK, N], F32, name="w2_raw", align_bytes=64)
-        w2_rows = w2.rearrange("(b t r) n -> t b r n", t=PACK, r=8)
+        w2_rows = w2.rearrange("(b t r) n -> t b r n", t=PACK, r=BLOCK_PARTITIONS)
         for t in range(PACK):
             nc.sync.dma_start(out=w2_raw[:, t, :], in_=w2_rows[t])
         gate_sb = keep.tile([P, V], F32, name="gate_sb", align_bytes=64)
@@ -86,15 +97,16 @@ def tile_picked_vpool_relu_p_kernel(
         nc.vector.tensor_copy(x_scale[:], scale_table[:].indirect(offs_sb[:]))
 
         w1_bf = [
-            reuse.tile([P, PACK, P, PACK], BF16, name="w1_bf0", offset=0, align_bytes=64),
-            keep.tile([P, PACK, P, PACK], BF16, name="w1_bf1", tag="w1_bf1", align_bytes=64),
+            keep.tile([P, PACK, P, PACK], BF16, name="w1_bf0", tag="w1_bf0", align_bytes=64),
+            reuse.tile([P, PACK, P, PACK], BF16, name="w1_bf1", offset=0, align_bytes=64),
         ]
         w1_codes = {}
-        w1_scale = [keep.tile([P, H], U8, name="w1_scale%d" % o, align_bytes=64) for o in range(2)]
+        w1_scale = [keep.tile([P, H], U8, name="w1_scale%d" % o, align_bytes=64) for o in range(PASSES)]
 
         def deal_views(o, t):
-            dst = w1_bf[o][:, t].rearrange("p (b h i) j -> p b h j i", h=2, i=4)
-            src = w1_raw[o][:].rearrange("p j (b t h i) -> p t b h j i", t=PACK, h=2, i=4)[:, t]
+            lines = BLOCK_PARTITIONS // LINE
+            dst = w1_bf[o][:, t].rearrange("p (b h e) j -> p b h j e", h=lines, e=LINE)
+            src = w1_raw[o][:].rearrange("p j (b t h e) -> p t b h j e", t=PACK, h=lines, e=LINE)[:, t]
             return dst, src
 
         def quantize_w1(o, tag):
@@ -106,80 +118,75 @@ def tile_picked_vpool_relu_p_kernel(
             )
 
         for t in range(PACK):
-            nc.scalar.copy(*deal_views(1, t))
-        quantize_w1(1, "scale_table")
+            nc.scalar.copy(*deal_views(0, t))
+        quantize_w1(0, "scale_table")
         for t in range(PACK):
             if t < SCALAR_TILES:
-                nc.scalar.copy(*deal_views(0, t))
+                nc.scalar.copy(*deal_views(1, t))
             else:
-                nc.vector.tensor_copy(*deal_views(0, t))
-        quantize_w1(0, "w1_bf1")
+                nc.vector.tensor_copy(*deal_views(1, t))
+        quantize_w1(1, "w1_bf0")
 
         words1 = []
         for first, last in GATHER_PIECES:
             piece = reuse.tile(
-                [P, last - first], U32, name="words1_%d" % first, offset=4 * first, align_bytes=64
+                [P, last - first], U32, name="words1_%d" % first, offset=WORD_BYTES * first, align_bytes=64
             )
-            nc.vector.tensor_copy(piece[:], word_table[1][:].indirect(offs_sb[:, first // 16 : last // 16]))
+            entries = offs_sb[:, first // LIST_ROWS : last // LIST_ROWS]
+            nc.vector.tensor_copy(piece[:], word_table[1][:].indirect(entries))
             words1.extend(piece[:, n : n + BANK_TOKENS] for n in range(0, last - first, BANK_TOKENS))
 
-        w2_bf = keep.tile([P, N, PACK], BF16, name="w2_bf", tag="w1_raw0", align_bytes=64)
-        nc.scalar.activation(
-            w2_bf[:].rearrange("p (c i) j -> p c j i", i=4),
-            w2_raw[:].rearrange("p j (c i) -> p c j i", i=4),
-            ACT.Copy,
-        )
-        w2_codes = keep.tile([P, N], U32, name="w2_codes", tag="word_table1", align_bytes=64)
-        w2_scale = keep.tile([P, N], U8, name="w2_scale", align_bytes=64)
-        nc.vector.quantize_mx(
-            out=w2_codes[:].bitcast(FP8X4), scales=w2_scale[:], in_=w2_bf[:].rearrange("p n j -> p (n j)")
-        )
-
-        def first_pass(bank, b, t, o):
-            tok = slice(b * BANK_TOKENS, (b + 1) * BANK_TOKENS)
-            if o == 0:
-                rhs = words0[:, tok]
-            else:
-                rhs = words1[b]
+        def first_product_pass(bank, b, t, o):
+            tokens = slice(b * BANK_TOKENS, (b + 1) * BANK_TOKENS)
+            moving = words0[:, tokens] if o == 0 else words1[b]
             nc.tensor.matmul_mx(
                 out=bank[:, t, :],
                 lhsT=w1_codes[o][:, t * P : (t + 1) * P].bitcast(FP8X4),
                 lhsT_scale=w1_scale[o][:, t * P : (t + 1) * P],
-                rhs=rhs.bitcast(FP8X4),
-                rhs_scale=x_scale[4 * o : P, tok],
+                rhs=moving.bitcast(FP8X4),
+                rhs_scale=x_scale[SCALE_ROWS * o : P, tokens],
                 start=(o == 0),
-                stop=(o == 1),
+                stop=(o == PASSES - 1),
             )
 
-        warm_bank = psum.tile([P, 512], F32, name="warm_bank", tag="bank%d" % (BANKS - 1))
-        for i in range(4):
+        warm_bank = psum.tile([P, WARM_N], F32, name="warm_bank", tag="bank%d" % (BANKS - 1))
+
+        def warm_up():
             nc.tensor.matmul_mx(
                 out=warm_bank[:],
                 lhsT=words0[:, 0:P].bitcast(FP8X4),
                 lhsT_scale=x_scale[:, 0:P],
-                rhs=words0[:, 0:512].bitcast(FP8X4),
-                rhs_scale=x_scale[:, 0:512],
+                rhs=words0[:, 0:WARM_N].bitcast(FP8X4),
+                rhs_scale=x_scale[:, 0:WARM_N],
                 start=True,
                 stop=True,
             )
 
-        banks = []
-        for b in range(BANKS):
+        def open_bank(b):
             bank = psum.tile([P, PACK, BANK_TOKENS], F32, name="h_bank%d" % b, tag="bank%d" % b)
-            banks.append(bank)
-            first_pass(bank, b, 0, 0)
+            first_product_pass(bank, b, 0, 0)
+            return bank
 
-        h_bf = [keep.tile([P, D, CHUNK_V, PACK], BF16, name="h_bf%d" % c, tag="h_bf%d" % c, align_bytes=64) for c in range(CHUNKS)]
-        z_codes = keep.tile([P, V], U32, name="z_codes", align_bytes=64)
-        z_scale = keep.tile([P, V], U8, name="z_scale", align_bytes=64)
+        warm_up()
+        warm_up()
+        banks = [open_bank(b) for b in range(BANKS - 1)]
+        warm_up()
+        warm_up()
+
+        h_bf = [
+            keep.tile([P, D, CHUNK_V, PACK], BF16, name="h_bf%d" % c, tag="h_bf%d" % c, align_bytes=64)
+            for c in range(CHUNKS)
+        ]
+        z_codes = [keep.tile([P, CHUNK_V], U32, name="z_codes%d" % c, align_bytes=64) for c in range(CHUNKS)]
+        z_scale = [keep.tile([P, CHUNK_V], U8, name="z_scale%d" % c, align_bytes=64) for c in range(CHUNKS)]
 
         def first_layer(b):
-            bank = banks[b]
-            first_pass(bank, b, 0, 1)
+            bank = banks[b] if b < BANKS - 1 else open_bank(b)
+            first_product_pass(bank, b, 0, 1)
             for t in range(1, PACK):
-                first_pass(bank, b, t, 0)
-                first_pass(bank, b, t, 1)
-            c, half = divmod(b, CHUNK_TOKENS // BANK_TOKENS)
+                first_product_pass(bank, b, t, 0)
+                first_product_pass(bank, b, t, 1)
+            c, half = divmod(b, CHUNK_V // BANK_V)
             nc.scalar.activation(
                 h_bf[c][:, :, half * BANK_V : (half + 1) * BANK_V, :].rearrange("p d v t -> p v t d"),
                 bank[:].rearrange("p t (v d) -> p v t d", d=D),
@@ -187,40 +194,60 @@ def tile_picked_vpool_relu_p_kernel(
             )
 
         def pool(c):
-            z_bf = keep.tile([P, CHUNK_V * PACK], BF16, name="z_bf%d" % c, align_bytes=64)
+            z_bf = keep.tile([P, CHUNK_V * PACK], BF16, name="z_bf%d" % c, tag="z_bf%d" % c, align_bytes=64)
             nc.vector.tensor_tensor(
                 z_bf[:],
                 h_bf[c][:, 0].rearrange("p v t -> p (v t)"),
                 h_bf[c][:, 1].rearrange("p v t -> p (v t)"),
                 ALU.max,
             )
-            cols = slice(c * CHUNK_V, (c + 1) * CHUNK_V)
-            nc.vector.quantize_mx(out=z_codes[:, cols].bitcast(FP8X4), scales=z_scale[:, cols], in_=z_bf[:])
+            nc.vector.quantize_mx(out=z_codes[c][:].bitcast(FP8X4), scales=z_scale[c][:], in_=z_bf[:])
 
-        def place(first, last, b, host):
-            y_bank = psum.tile([P, last - first], F32, name="y_bank%d" % first, tag="bank%d" % b)
+        w2_codes = keep.tile([P, N], U32, name="w2_codes", align_bytes=64)
+        w2_scale = keep.tile([P, N], U8, name="w2_scale", align_bytes=64)
+
+        def quantize_w2():
+            w2_bf = keep.tile([P, N, PACK], BF16, name="w2_bf", tag="z_bf0", align_bytes=64)
+            nc.vector.tensor_copy(
+                w2_bf[:].rearrange("p (h e) t -> p h t e", e=LINE),
+                w2_raw[:].rearrange("p t (h e) -> p h t e", e=LINE),
+            )
+            nc.vector.quantize_mx(
+                out=w2_codes[:].bitcast(FP8X4), scales=w2_scale[:], in_=w2_bf[:].rearrange("p n t -> p (n t)")
+            )
+
+        def second_layer(c):
+            y_bank = psum.tile([P, CHUNK_V], F32, name="y_bank%d" % c, tag="bank%d" % c)
             nc.tensor.matmul_mx(
                 out=y_bank[:],
                 lhsT=w2_codes[:].bitcast(FP8X4),
                 lhsT_scale=w2_scale[:],
-                rhs=z_codes[:, first:last].bitcast(FP8X4),
-                rhs_scale=z_scale[:, first:last],
+                rhs=z_codes[c][:].bitcast(FP8X4),
+                rhs_scale=z_scale[c][:],
                 start=True,
                 stop=True,
             )
-            y_sb = keep.tile([P, last - first], F32, name="y_sb%d" % first, tag=host, align_bytes=64)
-            nc.scalar.copy(y_sb[:], y_bank[:])
-            nc.vector.tensor_tensor(
-                frame[:].indirect(pos_sb[:, first // 16 : last // 16]), y_sb[:], gate_sb[:, first:last], ALU.mult
-            )
+            return y_bank
 
+        def place(c, y_bank, tag):
+            first, last = c * CHUNK_V, (c + 1) * CHUNK_V
+            y_sb = keep.tile([P, CHUNK_V], F32, name="y_sb%d" % c, tag=tag, align_bytes=64)
+            nc.scalar.copy(y_sb[:], y_bank[:])
+            entries = pos_sb[:, first // LIST_ROWS : last // LIST_ROWS]
+            nc.vector.tensor_tensor(frame[:].indirect(entries), y_sb[:], gate_sb[:, first:last], ALU.mult)
+
+        y_banks = {}
         for c in range(CHUNKS):
             first_layer(2 * c)
+            if c >= 2:
+                place(c - 2, y_banks[c - 2], "y_sb%d" % (c - 2))
             first_layer(2 * c + 1)
+            if c >= 1:
+                y_banks[c - 1] = second_layer(c - 1)
             pool(c)
-            if c == 1:
-                place(*GROUPS[0])
-        place(*GROUPS[1])
-        place(*GROUPS[2])
+            if c == 0:
+                quantize_w2()
+        place(CHUNKS - 2, y_banks[CHUNKS - 2], "h_bf%d" % (CHUNKS - 1))
+        place(CHUNKS - 1, second_layer(CHUNKS - 1), "y_sb%d" % (CHUNKS - 1))
 
         nc.sync.dma_start(out=out, in_=frame[:])

from contextlib import ExitStack

import concourse.mybir as mybir

K, T, D, S, V, H, N = 1024, 2048, 2, 1024, 512, 512, 128
FLOPS = 2 * K * H * S + 2 * H * N * V

F32 = mybir.dt.float32
BF16 = mybir.dt.bfloat16
I32 = mybir.dt.int32
U32 = mybir.dt.uint32
U16 = mybir.dt.uint16
U8 = mybir.dt.uint8
FP8X4 = mybir.dt.float8_e4m3fn_x4
ACT = mybir.ActivationFunctionType
ALU = mybir.AluOpType

P = 128
PACK = 4
K_PASS = P * PACK
PASSES = K // K_PASS
QUADRANT = 32
SCALE_ROWS = 4
BLOCK_PARTITIONS = 8
LINE = 4
LIST_ROWS = 16
WORD_BYTES = 4

BANK_TOKENS = 128
BANKS = S // BANK_TOKENS
BANK_V = BANK_TOKENS // D
CHUNK_V = 2 * BANK_V
CHUNKS = V // CHUNK_V
WARM_N = 512

SCALAR_TILES = 2
GATHER_PIECES = ((0, 256), (256, 512), (512, 1024))


def tile_picked_vpool_relu_p_kernel(
    tc, x_words, x_scales, w1, w2, gate, offs, pos1, out
):
    nc = tc.nc
    with ExitStack() as ctx:
        keep = ctx.enter_context(tc.tile_pool(name="keep", bufs=1))
        reuse = ctx.enter_context(tc.tile_pool(name="reuse", bufs=1))
        psum = ctx.enter_context(tc.psum_pool(name="psum", bufs=1))

        offs_sb = keep.tile([P, S // LIST_ROWS], U16, name="offs_sb")
        pos_sb = keep.tile([P, V // LIST_ROWS], U16, name="pos_sb")

        scale_table = keep.tile([P, T], U8, name="scale_table", tag="scale_table", align_bytes=64)
        nc.vector.memset(scale_table[:].bitcast(I32), 0)

        word_table = [
            keep.tile([P, T], U32, name="word_table%d" % o, tag="word_table%d" % o, align_bytes=64)
            for o in range(PASSES)
        ]
        w1_raw = [keep.tile([P, PACK, H], F32, name="w1_raw%d" % o, align_bytes=64) for o in range(PASSES)]

        def load_words(o):
            nc.sync.dma_start(
                out=word_table[o][:].bitcast(I32),
                in_=x_words[o].rearrange("p c r -> p (c r)").bitcast(I32),
            )

        def load_w1(o):
            nc.sync.dma_start(
                out=w1_raw[o][:],
                in_=w1[o * K_PASS : (o + 1) * K_PASS, :].rearrange("(p j) c -> p j c", j=PACK),
            )

        load_words(0)
        nc.sync.dma_start(offs_sb[:], offs)
        nc.sync.dma_start(pos_sb[:], pos1)
        for q in range(P // QUADRANT):
            nc.sync.dma_start(
                out=scale_table[QUADRANT * q : QUADRANT * q + PASSES * SCALE_ROWS, :].bitcast(I32),
                in_=x_scales[:, SCALE_ROWS * q : SCALE_ROWS * (q + 1), :].bitcast(I32),
            )
        load_w1(0)
        load_w1(1)
        load_words(1)
        w2_raw = keep.tile([P, PACK, N], F32, name="w2_raw", align_bytes=64)
        w2_rows = w2.rearrange("(b t r) n -> t b r n", t=PACK, r=BLOCK_PARTITIONS)
        for t in range(PACK):
            nc.sync.dma_start(out=w2_raw[:, t, :], in_=w2_rows[t])
        gate_sb = keep.tile([P, V], F32, name="gate_sb", align_bytes=64)
        nc.sync.dma_start(out=gate_sb[:], in_=gate)

        frame = keep.tile([P, 2 * V], F32, name="frame", align_bytes=64)
        nc.vector.memset(frame[:], 0.0)

        words0 = keep.tile([P, S], U32, name="words0", align_bytes=64)
        nc.vector.tensor_copy(words0[:], word_table[0][:].indirect(offs_sb[:]))
        x_scale = keep.tile([P, S], U8, name="x_scale", tag="word_table0", align_bytes=64)
        nc.vector.tensor_copy(x_scale[:], scale_table[:].indirect(offs_sb[:]))

        w1_bf = [
            keep.tile([P, PACK, P, PACK], BF16, name="w1_bf0", tag="w1_bf0", align_bytes=64),
            reuse.tile([P, PACK, P, PACK], BF16, name="w1_bf1", offset=0, align_bytes=64),
        ]
        w1_codes = {}
        w1_scale = [keep.tile([P, H], U8, name="w1_scale%d" % o, align_bytes=64) for o in range(PASSES)]

        def deal_views(o, t):
            lines = BLOCK_PARTITIONS // LINE
            dst = w1_bf[o][:, t].rearrange("p (b h e) j -> p b h j e", h=lines, e=LINE)
            src = w1_raw[o][:].rearrange("p j (b t h e) -> p t b h j e", t=PACK, h=lines, e=LINE)[:, t]
            return dst, src

        def quantize_w1(o, tag):
            w1_codes[o] = keep.tile([P, H], U32, name="w1_codes%d" % o, tag=tag, align_bytes=64)
            nc.vector.quantize_mx(
                out=w1_codes[o][:].bitcast(FP8X4),
                scales=w1_scale[o][:],
                in_=w1_bf[o][:].rearrange("p t m j -> p (t m j)"),
            )

        for t in range(PACK):
            nc.scalar.copy(*deal_views(0, t))
        quantize_w1(0, "scale_table")
        for t in range(PACK):
            if t < SCALAR_TILES:
                nc.scalar.copy(*deal_views(1, t))
            else:
                nc.vector.tensor_copy(*deal_views(1, t))
        quantize_w1(1, "w1_bf0")

        words1 = []
        for first, last in GATHER_PIECES:
            piece = reuse.tile(
                [P, last - first], U32, name="words1_%d" % first, offset=WORD_BYTES * first, align_bytes=64
            )
            entries = offs_sb[:, first // LIST_ROWS : last // LIST_ROWS]
            nc.vector.tensor_copy(piece[:], word_table[1][:].indirect(entries))
            words1.extend(piece[:, n : n + BANK_TOKENS] for n in range(0, last - first, BANK_TOKENS))

        def first_product_pass(bank, b, t, o):
            tokens = slice(b * BANK_TOKENS, (b + 1) * BANK_TOKENS)
            moving = words0[:, tokens] if o == 0 else words1[b]
            nc.tensor.matmul_mx(
                out=bank[:, t, :],
                lhsT=w1_codes[o][:, t * P : (t + 1) * P].bitcast(FP8X4),
                lhsT_scale=w1_scale[o][:, t * P : (t + 1) * P],
                rhs=moving.bitcast(FP8X4),
                rhs_scale=x_scale[SCALE_ROWS * o : P, tokens],
                start=(o == 0),
                stop=(o == PASSES - 1),
            )

        warm_bank = psum.tile([P, WARM_N], F32, name="warm_bank", tag="bank%d" % (BANKS - 1))

        def warm_up():
            nc.tensor.matmul_mx(
                out=warm_bank[:],
                lhsT=words0[:, 0:P].bitcast(FP8X4),
                lhsT_scale=x_scale[:, 0:P],
                rhs=words0[:, 0:WARM_N].bitcast(FP8X4),
                rhs_scale=x_scale[:, 0:WARM_N],
                start=True,
                stop=True,
            )

        def open_bank(b):
            bank = psum.tile([P, PACK, BANK_TOKENS], F32, name="h_bank%d" % b, tag="bank%d" % b)
            first_product_pass(bank, b, 0, 0)
            return bank

        warm_up()
        warm_up()
        banks = [open_bank(b) for b in range(BANKS - 1)]
        warm_up()
        warm_up()

        h_bf = [
            keep.tile([P, D, CHUNK_V, PACK], BF16, name="h_bf%d" % c, tag="h_bf%d" % c, align_bytes=64)
            for c in range(CHUNKS)
        ]
        z_codes = [keep.tile([P, CHUNK_V], U32, name="z_codes%d" % c, align_bytes=64) for c in range(CHUNKS)]
        z_scale = [keep.tile([P, CHUNK_V], U8, name="z_scale%d" % c, align_bytes=64) for c in range(CHUNKS)]

        def first_layer(b):
            bank = banks[b] if b < BANKS - 1 else open_bank(b)
            first_product_pass(bank, b, 0, 1)
            for t in range(1, PACK):
                first_product_pass(bank, b, t, 0)
                first_product_pass(bank, b, t, 1)
            c, half = divmod(b, CHUNK_V // BANK_V)
            nc.scalar.activation(
                h_bf[c][:, :, half * BANK_V : (half + 1) * BANK_V, :].rearrange("p d v t -> p v t d"),
                bank[:].rearrange("p t (v d) -> p v t d", d=D),
                ACT.Relu,
            )

        def pool(c):
            z_bf = keep.tile([P, CHUNK_V * PACK], BF16, name="z_bf%d" % c, tag="z_bf%d" % c, align_bytes=64)
            nc.vector.tensor_tensor(
                z_bf[:],
                h_bf[c][:, 0].rearrange("p v t -> p (v t)"),
                h_bf[c][:, 1].rearrange("p v t -> p (v t)"),
                ALU.max,
            )
            nc.vector.quantize_mx(out=z_codes[c][:].bitcast(FP8X4), scales=z_scale[c][:], in_=z_bf[:])

        w2_codes = keep.tile([P, N], U32, name="w2_codes", align_bytes=64)
        w2_scale = keep.tile([P, N], U8, name="w2_scale", align_bytes=64)

        def quantize_w2():
            w2_bf = keep.tile([P, N, PACK], BF16, name="w2_bf", tag="z_bf0", align_bytes=64)
            nc.vector.tensor_copy(
                w2_bf[:].rearrange("p (h e) t -> p h t e", e=LINE),
                w2_raw[:].rearrange("p t (h e) -> p h t e", e=LINE),
            )
            nc.vector.quantize_mx(
                out=w2_codes[:].bitcast(FP8X4), scales=w2_scale[:], in_=w2_bf[:].rearrange("p n t -> p (n t)")
            )

        def second_layer(c):
            y_bank = psum.tile([P, CHUNK_V], F32, name="y_bank%d" % c, tag="bank%d" % c)
            nc.tensor.matmul_mx(
                out=y_bank[:],
                lhsT=w2_codes[:].bitcast(FP8X4),
                lhsT_scale=w2_scale[:],
                rhs=z_codes[c][:].bitcast(FP8X4),
                rhs_scale=z_scale[c][:],
                start=True,
                stop=True,
            )
            return y_bank

        def place(c, y_bank, tag):
            first, last = c * CHUNK_V, (c + 1) * CHUNK_V
            y_sb = keep.tile([P, CHUNK_V], F32, name="y_sb%d" % c, tag=tag, align_bytes=64)
            nc.scalar.copy(y_sb[:], y_bank[:])
            entries = pos_sb[:, first // LIST_ROWS : last // LIST_ROWS]
            nc.vector.tensor_tensor(frame[:].indirect(entries), y_sb[:], gate_sb[:, first:last], ALU.mult)

        y_banks = {}
        for c in range(CHUNKS):
            first_layer(2 * c)
            if c >= 2:
                place(c - 2, y_banks[c - 2], "y_sb%d" % (c - 2))
            first_layer(2 * c + 1)
            if c >= 1:
                y_banks[c - 1] = second_layer(c - 1)
            pool(c)
            if c == 0:
                quantize_w2()
        place(CHUNKS - 2, y_banks[CHUNKS - 2], "h_bf%d" % (CHUNKS - 1))
        place(CHUNKS - 1, second_layer(CHUNKS - 1), "y_sb%d" % (CHUNKS - 1))

        nc.sync.dma_start(out=out, in_=frame[:])
